import numpy as np
import ml_dtypes


def mxq(x, axis, fmt="e4m3"):
    dtype, down = {"e4m3": (ml_dtypes.float8_e4m3fn, 7), "e5m2": (ml_dtypes.float8_e5m2, 14)}[fmt]
    v = np.moveaxis(np.asarray(x, np.float32).astype(ml_dtypes.bfloat16).astype(np.float64), axis, -1)
    blocks = v.reshape(v.shape[:-1] + (-1, 32))
    amax = np.abs(blocks).max(-1, keepdims=True)
    byte = np.maximum(np.where(amax > 0, np.frexp(amax)[1] - 1 + 127, 0) - down, 1)
    scale = np.exp2(byte - 127.0)
    codes = (blocks / scale).astype(np.float32).astype(dtype).astype(np.float64)
    return np.moveaxis((codes * scale).reshape(v.shape), -1, axis)


WIDE = False


def mx_kscale(k):
    if not WIDE:
        return np.ones(k)
    levels = np.array([10, -10, 5, -5, 0])
    if k % 512:
        return np.exp2(np.random.permutation(np.resize(levels, k // 32))).repeat(32)
    a = np.empty((k // 512, 16))
    for p in range(k // 512):
        a[p, :8] = np.random.permutation(np.resize(levels, 8))
        for g in range(8):
            far = levels[np.abs(levels - a[p, g]) >= 10]
            a[p, g + 8] = far[np.random.randint(len(far))]
    return np.exp2(a.ravel()).repeat(32)


def f64(x):
    return np.asarray(x).astype(np.float64)


def striped(idx):
    return np.tile(idx.reshape(-1, 16).T, (8, 1)).astype(np.uint16)


def unstriped(offs):
    return offs[:16].T.reshape(-1).astype(np.int64)


def striped8(idx):
    return np.concatenate([x.reshape(-1, 16).T for x in idx]).astype(np.uint16)


def runs(offs, k):
    lists = np.stack([offs[16 * r : 16 * r + 16].T.reshape(-1) for r in range(8)]).astype(np.int64)
    return lists[np.arange(k) % 512 // 64]


def pack_weight(w):
    k, n = w.shape
    w = f64(np.asarray(w, np.float32).astype(ml_dtypes.bfloat16)).reshape(k // 32, 32, n)
    amax = np.abs(w).max(1)
    byte = np.clip(np.where(amax > 0, np.frexp(amax)[1] - 1 + 127 - 7, 1), 1, 254)
    scaled = (w * np.exp2(127.0 - byte)[:, None, :]).reshape(k, n).astype(np.float32)
    words = np.ascontiguousarray(scaled.reshape(k // 512, 128, 4, n).transpose(0, 1, 3, 2)).astype(ml_dtypes.float8_e4m3fn).view(np.uint8)
    return words, np.ascontiguousarray(byte.astype(np.uint8).reshape(k // 512, 16, n))


def unpack_weight(words, scales):
    g, p, n, _ = words.shape
    vals = np.ascontiguousarray(words).view(ml_dtypes.float8_e4m3fn).astype(np.float64) * np.repeat(np.exp2(scales.astype(np.float64) - 127.0), 8, axis=1)[..., None]
    return vals.transpose(0, 1, 3, 2).reshape(g * 512, n)


K, T, S, N, G, H = 512, 1024, 512, 512, 2048, 512


def setup_inputs():
    n = np.random.standard_normal
    s = mx_kscale(K)[:, None]
    u = mx_kscale(S)
    packed_xT = pack_weight(n((K, T)) * s)
    packed_dT = pack_weight(n((K, G)) / s)
    return {
        "x_words": packed_xT[0],
        "x_scales": packed_xT[1],
        "d_words": packed_dT[0],
        "d_scales": packed_dT[1],
        "gn": (np.random.uniform(0.5, 1.5, (H, 1)) * u[:, None]).astype(np.float32),
        "w1": (n((H, N)) / np.sqrt(H) / u[:, None]).astype(np.float32),
        "offs": striped(np.random.permutation(T)[:S]),
        "k1": striped8(np.random.randint(0, G, (8, H))),
        "two": striped(np.random.permutation(T)[:S]),
        "k2": striped8(np.random.randint(0, G, (8, H))),
        "n1": striped8(np.stack([np.random.permutation(S) for _ in range(8)])),
        "n2": striped8(np.stack([np.random.permutation(S) for _ in range(8)])),
        "n3": striped8(np.stack([np.random.permutation(S) for _ in range(8)])),
        "n4": striped8(np.stack([np.random.permutation(S) for _ in range(8)])),
    }


def reference(x_words, x_scales, d_words, d_scales, gn, w1, offs, k1, two, k2, n1, n2, n3, n4):
    d_k1 = unpack_weight(d_words, d_scales)[np.arange(K)[:, None], runs(k1, K)]
    xq = unpack_weight(x_words, x_scales)[:, unstriped(offs)]
    a = 0.0625 * (d_k1.T @ xq)
    d_k2 = unpack_weight(d_words, d_scales)[np.arange(K)[:, None], runs(k2, K)]
    x_two = unpack_weight(x_words, x_scales)[:, unstriped(two)]
    b = 0.0625 * (d_k2.T @ x_two)
    z = f64(gn) * (a * (np.tanh(b[np.arange(H)[:, None], runs(n1, H)] - (b[np.arange(H)[:, None], runs(n2, H)]))))
    h = mxq(f64(w1), 0, "e4m3").T @ mxq(z, 0, "e4m3")
    pa = h[np.arange(N)[:, None], runs(n3, N)]
    pb = h[np.arange(N)[:, None], runs(n4, N)]
    return np.maximum(np.maximum(h, pa), pb) - (0.5 * (np.minimum(np.minimum(h, pa), pb)))

@@ -1,0 +1,197 @@
+from contextlib import ExitStack
+
+import concourse.mybir as mybir
+
+F32 = mybir.dt.float32
+BF16 = mybir.dt.bfloat16
+I32 = mybir.dt.int32
+U32 = mybir.dt.uint32
+U16 = mybir.dt.uint16
+U8 = mybir.dt.uint8
+FP8X4 = mybir.dt.float8_e4m3fn_x4
+ALU = mybir.AluOpType
+ACT = mybir.ActivationFunctionType
+
+P = 128
+T, G, S = 1024, 2048, 512
+TILES = 4
+HALF = 256
+FLOPS = 3 * 2 * 512 * 512 * 512
+
+
+def tile_picked_twpqjointbrange_none_p_kernel(tc, x_words, x_scales, d_words, d_scales, gn, w1, offs, k1, two, k2, n1, n2, n3, n4, out):
+    nc = tc.nc
+    with ExitStack() as ctx:
+        sb = ctx.enter_context(tc.tile_pool(name="sb", bufs=1))
+        ps = ctx.enter_context(tc.psum_pool(name="ps", bufs=1))
+
+        def tile(name, shape, dtype):
+            return sb.tile(shape, dtype, name=name, align_bytes=64)
+
+        def load_list(name, src):
+            t = sb.tile([P, S // 16], U16, name=name)
+            nc.sync.dma_start(t[:], src)
+            return t
+
+        d_bytes = tile("d_bytes", [P, G], U8)
+        x_bytes = tile("x_bytes", [P, T], U8)
+        nc.vector.memset(x_bytes[:].bitcast(I32), 0)
+
+        l_k2 = load_list("l_k2", k2)
+        d_rows = d_scales[0].bitcast(I32).rearrange("(r e) c -> e r c", e=2)
+        for e in range(2):
+            nc.sync.dma_start(d_bytes[e:P:2, :].bitcast(I32), d_rows[e].unsqueeze(1).to_broadcast([8, 8, G // 4]))
+        l_two = load_list("l_two", two)
+        l_n1 = load_list("l_n1", n1)
+        l_n2 = load_list("l_n2", n2)
+        x_tab = tile("x_tab", [P, T], U32)
+        nc.sync.dma_start(x_tab[:].bitcast(I32), x_words[0].rearrange("p n t -> p (n t)").bitcast(I32))
+        d_tab = tile("d_tab", [P, G], U32)
+        nc.sync.dma_start(d_tab[:].bitcast(I32), d_words[0].rearrange("p n t -> p (n t)").bitcast(I32))
+        x_rows = x_scales[0].rearrange("(q s) c -> s q c", s=4)
+        for s in range(4):
+            nc.sync.dma_start(x_bytes[s:P:32, :].bitcast(I32), x_rows[s].bitcast(I32))
+
+        def deal(dst, src, run):
+            nc.vector.tensor_copy(out=dst.rearrange("p (t b q) -> p t b q", t=TILES, q=run),
+                                  in_=src.rearrange("p (b t q) -> p t b q", t=TILES, q=run))
+
+        def pick_scales(name, codes, queue):
+            got = tile(name + "_sg", [P, S], U8)
+            nc.vector.tensor_copy(out=got[:], in_=d_bytes[:].indirect(codes[:]))
+            odd = tile(name + "_so", [P, S], U8)
+            plane = tile(name + "_sp", [P, S], U8)
+            deal(odd[:].bitcast(I32), got[:].bitcast(I32), 2)
+            deal(plane[:].bitcast(I32), got[:].bitcast(I32), 2)
+            for e in range(2):
+                queue.dma_start(plane[2 + e:P:32, :].bitcast(I32), odd[16 + e:P:32, :].bitcast(I32))
+            return plane
+
+        def pick_words(name, codes):
+            got = tile(name + "_wg", [P, S], U32)
+            nc.vector.tensor_copy(out=got[:], in_=d_tab[:].indirect(codes[:]))
+            dealt = tile(name + "_wd", [P, S], U32)
+            deal(dealt[:], got[:], 8)
+            return dealt
+
+        def pick_token_words(name, tokens):
+            words = tile(name + "_xw", [P, S], U32)
+            nc.vector.tensor_copy(out=words[:], in_=x_tab[:].indirect(tokens[:]))
+            return words
+
+        def pick_token_scales(name, tokens):
+            scales = tile(name + "_xs", [P, S], U8)
+            nc.vector.tensor_copy(out=scales[:], in_=x_bytes[:].indirect(tokens[:]))
+            return scales
+
+        def product(dst, lw, ls, t, rw, rs):
+            cols = slice(t * P, (t + 1) * P)
+            nc.tensor.matmul_mx(out=dst, lhsT=lw[:, cols].bitcast(FP8X4), lhsT_scale=ls[:, cols],
+                                rhs=rw.bitcast(FP8X4), rhs_scale=rs, start=True, stop=True)
+
+        b_ds = pick_scales("b", l_k2, nc.scalar)
+        b_xw = pick_token_words("b", l_two)
+        b_dw = pick_words("b", l_k2)
+        b_xs = pick_token_scales("b", l_two)
+
+        l_k1 = load_list("l_k1", k1)
+        l_offs = load_list("l_offs", offs)
+        w_raw = tile("w_raw", [P, TILES, S], F32)
+        w_rows = w1.rearrange("(b j q) c -> j b q c", j=TILES, q=8)
+        for j in range(TILES):
+            nc.sync.dma_start(w_raw[:, j, :], w_rows[j])
+        gain = tile("gain", [P, TILES, 8], F32)
+        g_rows = gn.rearrange("(b j q) o -> j b q o", j=TILES, q=8)
+        for j in range(TILES):
+            nc.sync.dma_start(gain[:, j, 0:1], g_rows[j])
+        l_n3 = load_list("l_n3", n3)
+        l_n4 = load_list("l_n4", n4)
+
+        b_win = []
+        for t in range(TILES):
+            bank = ps.tile([P, S], F32, name=f"b_ps{t}", tag=f"bank{t}")
+            product(bank[:], b_dw, b_ds, t, b_xw[:], b_xs[:])
+            win = tile(f"b_win{t}", [P, S], F32)
+            nc.scalar.activation(out=win[:], in_=bank[:], func=ACT.Copy, scale=0.0625)
+            b_win.append(win)
+
+        a_ds = pick_scales("a", l_k1, nc.sync)
+        a_dw = pick_words("a", l_k1)
+        a_xw = pick_token_words("a", l_offs)
+        a_xs = pick_token_scales("a", l_offs)
+        a_ps = []
+        for t in range(TILES):
+            bank = ps.tile([P, S], F32, name=f"a_ps{t}", tag=f"bank{TILES + t}")
+            product(bank[:], a_dw, a_ds, t, a_xw[:], a_xs[:])
+            a_ps.append(bank)
+
+        gain16 = tile("gain16", [P, TILES], F32)
+        nc.gpsimd.tensor_scalar(out=gain16[:], in0=gain[:, :, 0], scalar1=0.0625, scalar2=0.0, op0=ALU.mult, op1=ALU.add)
+
+        h_ps = [ps.tile([P, S], F32, name=f"h_ps{t}", tag=f"bank{t}") for t in range(TILES)]
+        h_win = [tile(f"h_win{t}", [P, S], F32) for t in range(TILES)]
+
+        def offsets(lst, c):
+            return lst[:, c * HALF // 16:(c + 1) * HALF // 16]
+
+        for c in range(2):
+            cols = slice(c * HALF, (c + 1) * HALF)
+            z_rows = tile(f"z_rows{c}", [P, TILES, HALF], BF16)
+            for t in range(TILES):
+                first = tile(f"first{c}_{t}", [P, HALF], F32)
+                diff = tile(f"diff{c}_{t}", [P, HALF], F32)
+                nc.scalar.activation(out=first[:], in_=b_win[t][:].indirect(offsets(l_n1, c)), func=ACT.Copy)
+                if (t < 2) == (c == 0):
+                    second = tile(f"second{c}_{t}", [P, HALF], F32)
+                    nc.scalar.activation(out=second[:], in_=b_win[t][:].indirect(offsets(l_n2, c)), func=ACT.Copy)
+                    nc.gpsimd.tensor_tensor(out=diff[:], in0=second[:], in1=first[:], op=ALU.subtract)
+                else:
+                    nc.vector.tensor_tensor(out=diff[:], in0=b_win[t][:].indirect(offsets(l_n2, c)), in1=first[:], op=ALU.subtract)
+                th = tile(f"th{c}_{t}", [P, HALF], F32)
+                nc.scalar.activation(out=th[:], in_=diff[:], func=ACT.Tanh, scale=-1.0)
+                nc.vector.scalar_tensor_tensor(out=z_rows[:, t, :], in0=a_ps[t][:, cols], scalar=gain16[:, t:t + 1], in1=th[:],
+                                               op0=ALU.mult, op1=ALU.mult)
+            if c == 0:
+                w_bf = tile("w_bf", [P, TILES, 16, 8, 4], BF16)
+                w_view = w_raw[:].rearrange("p j (b t q) -> p t b q j", t=TILES, q=8)
+                for t in range(TILES):
+                    nc.gpsimd.tensor_scalar(out=w_bf[:, t], in0=w_view[:, t], scalar1=1.0, scalar2=0.0, op0=ALU.mult, op1=ALU.add)
+                w_codes = tile("w_codes", [P, S], U32)
+                w_plane = tile("w_plane", [P, S], U8)
+                nc.vector.quantize_mx(out=w_codes[:].bitcast(FP8X4), scales=w_plane[:], in_=w_bf[:].rearrange("p t b q j -> p (t b q j)"))
+            z_bf = tile(f"z_bf{c}", [P, HALF, TILES], BF16)
+            nc.vector.tensor_copy(out=z_bf[:], in_=z_rows[:].rearrange("p t j -> p j t"))
+            z_codes = tile(f"z_codes{c}", [P, HALF], U32)
+            z_plane = tile(f"z_plane{c}", [P, HALF], U8)
+            nc.vector.quantize_mx(out=z_codes[:].bitcast(FP8X4), scales=z_plane[:], in_=z_bf[:].rearrange("p j t -> p (j t)"))
+            for t in range(TILES):
+                product(h_ps[t][:, cols], w_codes, w_plane, t, z_codes[:], z_plane[:])
+                nc.scalar.activation(out=h_win[t][:, cols], in_=h_ps[t][:, cols], func=ACT.Copy, scale=0.5)
+
+        out_rows = out.rearrange("(b t q) j -> t b q j", t=TILES, q=8)
+        for t in range(TILES):
+            pa = tile(f"pa{t}", [P, S], F32)
+            pb = tile(f"pb{t}", [P, S], F32)
+            for c in range(2):
+                cols = slice(c * HALF, (c + 1) * HALF)
+                if t == 0:
+                    nc.vector.tensor_copy(out=pa[:, cols], in_=h_win[t][:].indirect(offsets(l_n3, c)))
+                else:
+                    nc.scalar.activation(out=pa[:, cols], in_=h_win[t][:].indirect(offsets(l_n3, c)), func=ACT.Copy)
+            for c in range(2):
+                cols = slice(c * HALF, (c + 1) * HALF)
+                nc.scalar.activation(out=pb[:, cols], in_=h_win[t][:].indirect(offsets(l_n4, c)), func=ACT.Copy)
+            hi = tile(f"hi{t}", [P, S], F32)
+            lo = tile(f"lo{t}", [P, S], F32)
+            top = tile(f"top{t}", [P, S], F32)
+            low = tile(f"low{t}", [P, S], F32)
+            res = tile(f"res{t}", [P, S], F32)
+            nc.vector.scalar_tensor_tensor(out=hi[:], in0=pa[:], scalar=2.0, in1=h_ps[t][:], op0=ALU.mult, op1=ALU.max)
+            nc.vector.scalar_tensor_tensor(out=lo[:], in0=h_ps[t][:], scalar=0.5, in1=pa[:], op0=ALU.mult, op1=ALU.min)
+            pieces = [slice(0, S)] if t < TILES - 1 else [slice(0, HALF), slice(HALF, S)]
+            for cols in pieces:
+                nc.vector.scalar_tensor_tensor(out=top[:, cols], in0=pb[:, cols], scalar=2.0, in1=hi[:, cols], op0=ALU.mult, op1=ALU.max)
+                nc.vector.tensor_tensor(out=low[:, cols], in0=pb[:, cols], in1=lo[:, cols], op=ALU.min)
+                eng = nc.gpsimd if t < TILES - 1 else nc.vector
+                eng.tensor_tensor(out=res[:, cols], in0=top[:, cols], in1=low[:, cols], op=ALU.subtract)
+                nc.sync.dma_start(out_rows[t][:, :, cols], res[:, cols])

@@ -16,6 +16,7 @@ P = 128
 T, G, S = 1024, 2048, 512
 TILES = 4
 HALF = 256
+FUSED = ((0, 2), (0, 3), (1, 0), (1, 1))
 FLOPS = 3 * 2 * 512 * 512 * 512
 
 
@@ -25,8 +26,8 @@ def tile_picked_twpqjointbrange_none_p_kernel(tc, x_words, x_scales, d_words, d_
         sb = ctx.enter_context(tc.tile_pool(name="sb", bufs=1))
         ps = ctx.enter_context(tc.psum_pool(name="ps", bufs=1))
 
-        def tile(name, shape, dtype):
-            return sb.tile(shape, dtype, name=name, align_bytes=64)
+        def tile(name, shape, dtype, tag=None):
+            return sb.tile(shape, dtype, name=name, tag=tag or name, align_bytes=64)
 
         def load_list(name, src):
             t = sb.tile([P, S // 16], U16, name=name)
@@ -35,29 +36,26 @@ def tile_picked_twpqjointbrange_none_p_kernel(tc, x_words, x_scales, d_words, d_
 
         d_bytes = tile("d_bytes", [P, G], U8)
         x_bytes = tile("x_bytes", [P, T], U8)
-        nc.vector.memset(x_bytes[:].bitcast(I32), 0)
 
         l_k2 = load_list("l_k2", k2)
         d_rows = d_scales[0].bitcast(I32).rearrange("(r e) c -> e r c", e=2)
         for e in range(2):
             nc.sync.dma_start(d_bytes[e:P:2, :].bitcast(I32), d_rows[e].unsqueeze(1).to_broadcast([8, 8, G // 4]))
         l_two = load_list("l_two", two)
-        l_n1 = load_list("l_n1", n1)
-        l_n2 = load_list("l_n2", n2)
         x_tab = tile("x_tab", [P, T], U32)
         nc.sync.dma_start(x_tab[:].bitcast(I32), x_words[0].rearrange("p n t -> p (n t)").bitcast(I32))
+        x_rows = x_scales[0].bitcast(I32).rearrange("(q s) c -> q s c", s=4)
+        for q in range(4):
+            nc.sync.dma_start(x_bytes[32 * q:32 * (q + 1), :].bitcast(I32), x_rows[q].unsqueeze(0).to_broadcast([8, 4, T // 4]))
         d_tab = tile("d_tab", [P, G], U32)
         nc.sync.dma_start(d_tab[:].bitcast(I32), d_words[0].rearrange("p n t -> p (n t)").bitcast(I32))
-        x_rows = x_scales[0].rearrange("(q s) c -> s q c", s=4)
-        for s in range(4):
-            nc.sync.dma_start(x_bytes[s:P:32, :].bitcast(I32), x_rows[s].bitcast(I32))
 
         def deal(dst, src, run):
             nc.vector.tensor_copy(out=dst.rearrange("p (t b q) -> p t b q", t=TILES, q=run),
                                   in_=src.rearrange("p (b t q) -> p t b q", t=TILES, q=run))
 
-        def pick_scales(name, codes, queue):
-            got = tile(name + "_sg", [P, S], U8)
+        def pick_scales(name, codes, queue, tag):
+            got = tile(name + "_sg", [P, S], U8, tag)
             nc.vector.tensor_copy(out=got[:], in_=d_bytes[:].indirect(codes[:]))
             odd = tile(name + "_so", [P, S], U8)
             plane = tile(name + "_sp", [P, S], U8)
@@ -68,19 +66,19 @@ def tile_picked_twpqjointbrange_none_p_kernel(tc, x_words, x_scales, d_words, d_
             return plane
 
         def pick_words(name, codes):
-            got = tile(name + "_wg", [P, S], U32)
+            got = tile(name + "_wg", [P, S], U32, "picked")
             nc.vector.tensor_copy(out=got[:], in_=d_tab[:].indirect(codes[:]))
             dealt = tile(name + "_wd", [P, S], U32)
             deal(dealt[:], got[:], 8)
             return dealt
 
         def pick_token_words(name, tokens):
-            words = tile(name + "_xw", [P, S], U32)
+            words = tile(name + "_xw", [P, S], U32, "token_words")
             nc.vector.tensor_copy(out=words[:], in_=x_tab[:].indirect(tokens[:]))
             return words
 
         def pick_token_scales(name, tokens):
-            scales = tile(name + "_xs", [P, S], U8)
+            scales = tile(name + "_xs", [P, S], U8, "token_scales")
             nc.vector.tensor_copy(out=scales[:], in_=x_bytes[:].indirect(tokens[:]))
             return scales
 
@@ -89,11 +87,13 @@ def tile_picked_twpqjointbrange_none_p_kernel(tc, x_words, x_scales, d_words, d_
             nc.tensor.matmul_mx(out=dst, lhsT=lw[:, cols].bitcast(FP8X4), lhsT_scale=ls[:, cols],
                                 rhs=rw.bitcast(FP8X4), rhs_scale=rs, start=True, stop=True)
 
-        b_ds = pick_scales("b", l_k2, nc.scalar)
+        b_ds = pick_scales("b", l_k2, nc.scalar, "b_sg")
         b_xw = pick_token_words("b", l_two)
-        b_dw = pick_words("b", l_k2)
         b_xs = pick_token_scales("b", l_two)
+        b_dw = pick_words("b", l_k2)
 
+        l_n1 = load_list("l_n1", n1)
+        l_n2 = load_list("l_n2", n2)
         l_k1 = load_list("l_k1", k1)
         l_offs = load_list("l_offs", offs)
         w_raw = tile("w_raw", [P, TILES, S], F32)
@@ -115,7 +115,7 @@ def tile_picked_twpqjointbrange_none_p_kernel(tc, x_words, x_scales, d_words, d_
             nc.scalar.activation(out=win[:], in_=bank[:], func=ACT.Copy, scale=0.0625)
             b_win.append(win)
 
-        a_ds = pick_scales("a", l_k1, nc.sync)
+        a_ds = pick_scales("a", l_k1, nc.sync, "picked")
         a_dw = pick_words("a", l_k1)
         a_xw = pick_token_words("a", l_offs)
         a_xs = pick_token_scales("a", l_offs)
@@ -126,61 +126,64 @@ def tile_picked_twpqjointbrange_none_p_kernel(tc, x_words, x_scales, d_words, d_
             a_ps.append(bank)
 
         gain16 = tile("gain16", [P, TILES], F32)
-        nc.gpsimd.tensor_scalar(out=gain16[:], in0=gain[:, :, 0], scalar1=0.0625, scalar2=0.0, op0=ALU.mult, op1=ALU.add)
-
-        h_ps = [ps.tile([P, S], F32, name=f"h_ps{t}", tag=f"bank{t}") for t in range(TILES)]
-        h_win = [tile(f"h_win{t}", [P, S], F32) for t in range(TILES)]
+        nc.vector.tensor_scalar(out=gain16[:], in0=gain[:, :, 0], scalar1=0.0625, scalar2=None, op0=ALU.mult)
 
         def offsets(lst, c):
             return lst[:, c * HALF // 16:(c + 1) * HALF // 16]
 
+        z_q = []
         for c in range(2):
             cols = slice(c * HALF, (c + 1) * HALF)
             z_rows = tile(f"z_rows{c}", [P, TILES, HALF], BF16)
             for t in range(TILES):
                 first = tile(f"first{c}_{t}", [P, HALF], F32)
-                diff = tile(f"diff{c}_{t}", [P, HALF], F32)
+                diff = sb.tile([P, HALF], F32, name=f"diff{c}_{t}", tag=f"diff{c}_{t}", align_bytes=64)
                 nc.scalar.activation(out=first[:], in_=b_win[t][:].indirect(offsets(l_n1, c)), func=ACT.Copy)
-                if (t < 2) == (c == 0):
+                if (c, t) not in FUSED:
                     second = tile(f"second{c}_{t}", [P, HALF], F32)
                     nc.scalar.activation(out=second[:], in_=b_win[t][:].indirect(offsets(l_n2, c)), func=ACT.Copy)
-                    nc.gpsimd.tensor_tensor(out=diff[:], in0=second[:], in1=first[:], op=ALU.subtract)
+                    nc.vector.tensor_tensor(out=diff[:], in0=second[:], in1=first[:], op=ALU.subtract)
                 else:
                     nc.vector.tensor_tensor(out=diff[:], in0=b_win[t][:].indirect(offsets(l_n2, c)), in1=first[:], op=ALU.subtract)
                 th = tile(f"th{c}_{t}", [P, HALF], F32)
                 nc.scalar.activation(out=th[:], in_=diff[:], func=ACT.Tanh, scale=-1.0)
                 nc.vector.scalar_tensor_tensor(out=z_rows[:, t, :], in0=a_ps[t][:, cols], scalar=gain16[:, t:t + 1], in1=th[:],
                                                op0=ALU.mult, op1=ALU.mult)
-            if c == 0:
-                w_bf = tile("w_bf", [P, TILES, 16, 8, 4], BF16)
-                w_view = w_raw[:].rearrange("p j (b t q) -> p t b q j", t=TILES, q=8)
-                for t in range(TILES):
-                    nc.gpsimd.tensor_scalar(out=w_bf[:, t], in0=w_view[:, t], scalar1=1.0, scalar2=0.0, op0=ALU.mult, op1=ALU.add)
-                w_codes = tile("w_codes", [P, S], U32)
-                w_plane = tile("w_plane", [P, S], U8)
-                nc.vector.quantize_mx(out=w_codes[:].bitcast(FP8X4), scales=w_plane[:], in_=w_bf[:].rearrange("p t b q j -> p (t b q j)"))
             z_bf = tile(f"z_bf{c}", [P, HALF, TILES], BF16)
-            nc.vector.tensor_copy(out=z_bf[:], in_=z_rows[:].rearrange("p t j -> p j t"))
+            nc.vector.tensor_copy(out=z_bf[:].rearrange("p (c i) t -> p c t i", i=4), in_=z_rows[:].rearrange("p t (c i) -> p c t i", i=4))
             z_codes = tile(f"z_codes{c}", [P, HALF], U32)
             z_plane = tile(f"z_plane{c}", [P, HALF], U8)
             nc.vector.quantize_mx(out=z_codes[:].bitcast(FP8X4), scales=z_plane[:], in_=z_bf[:].rearrange("p j t -> p (j t)"))
-            for t in range(TILES):
-                product(h_ps[t][:, cols], w_codes, w_plane, t, z_codes[:], z_plane[:])
-                nc.scalar.activation(out=h_win[t][:, cols], in_=h_ps[t][:, cols], func=ACT.Copy, scale=0.5)
+            z_q.append((z_codes, z_plane))
 
+        w_bf = sb.tile([P, TILES, 16, 8, 4], BF16, name="w_bf", tag="diff1_3", align_bytes=64)
+        w_view = w_raw[:].rearrange("p j (b t q) -> p t b q j", t=TILES, q=8)
+        w_codes = tile("w_codes", [P, S], U32)
+        w_plane = tile("w_plane", [P, S], U8)
         out_rows = out.rearrange("(b t q) j -> t b q j", t=TILES, q=8)
+        h_ps, h_win = [], []
         for t in range(TILES):
+            rows = slice(t * P, (t + 1) * P)
+            nc.scalar.copy(out=w_bf[:, t], in_=w_view[:, t])
+            nc.vector.quantize_mx(out=w_codes[:, rows].bitcast(FP8X4), scales=w_plane[:, rows], in_=w_bf[:, t].rearrange("p b q j -> p (b q j)"))
+            bank = ps.tile([P, S], F32, name=f"h_ps{t}", tag=f"bank{t}")
+            for c in range(2):
+                product(bank[:, c * HALF:(c + 1) * HALF], w_codes, w_plane, t, z_q[c][0][:], z_q[c][1][:])
+            h_ps.append(bank)
+
+        for t in range(TILES):
+            win = tile(f"h_win{t}", [P, 2 * S], F32)
+            nc.scalar.activation(out=win[:, 0:S], in_=h_ps[t][:], func=ACT.Copy, scale=0.5)
+            h_win.append(win)
             pa = tile(f"pa{t}", [P, S], F32)
             pb = tile(f"pb{t}", [P, S], F32)
-            for c in range(2):
-                cols = slice(c * HALF, (c + 1) * HALF)
-                if t == 0:
-                    nc.vector.tensor_copy(out=pa[:, cols], in_=h_win[t][:].indirect(offsets(l_n3, c)))
-                else:
-                    nc.scalar.activation(out=pa[:, cols], in_=h_win[t][:].indirect(offsets(l_n3, c)), func=ACT.Copy)
-            for c in range(2):
-                cols = slice(c * HALF, (c + 1) * HALF)
-                nc.scalar.activation(out=pb[:, cols], in_=h_win[t][:].indirect(offsets(l_n4, c)), func=ACT.Copy)
+            if t == 0:
+                nc.vector.tensor_copy(out=pa[:], in_=h_win[t][:].indirect(l_n3[:]))
+            else:
+                nc.scalar.activation(out=pa[:], in_=h_win[t][:].indirect(l_n3[:]), func=ACT.Copy)
+            pieces = [slice(0, S)] if t < TILES - 1 else [slice(0, HALF), slice(HALF, S)]
+            for cols in pieces:
+                nc.scalar.activation(out=pb[:, cols], in_=h_win[t][:].indirect(l_n4[:, cols.start // 16:cols.stop // 16]), func=ACT.Copy)
             hi = tile(f"hi{t}", [P, S], F32)
             lo = tile(f"lo{t}", [P, S], F32)
             top = tile(f"top{t}", [P, S], F32)
@@ -188,10 +191,8 @@ def tile_picked_twpqjointbrange_none_p_kernel(tc, x_words, x_scales, d_words, d_
             res = tile(f"res{t}", [P, S], F32)
             nc.vector.scalar_tensor_tensor(out=hi[:], in0=pa[:], scalar=2.0, in1=h_ps[t][:], op0=ALU.mult, op1=ALU.max)
             nc.vector.scalar_tensor_tensor(out=lo[:], in0=h_ps[t][:], scalar=0.5, in1=pa[:], op0=ALU.mult, op1=ALU.min)
-            pieces = [slice(0, S)] if t < TILES - 1 else [slice(0, HALF), slice(HALF, S)]
             for cols in pieces:
                 nc.vector.scalar_tensor_tensor(out=top[:, cols], in0=pb[:, cols], scalar=2.0, in1=hi[:, cols], op0=ALU.mult, op1=ALU.max)
                 nc.vector.tensor_tensor(out=low[:, cols], in0=pb[:, cols], in1=lo[:, cols], op=ALU.min)
-                eng = nc.gpsimd if t < TILES - 1 else nc.vector
-                eng.tensor_tensor(out=res[:, cols], in0=top[:, cols], in1=low[:, cols], op=ALU.subtract)
+                nc.vector.tensor_tensor(out=res[:, cols], in0=top[:, cols], in1=low[:, cols], op=ALU.subtract)
                 nc.sync.dma_start(out_rows[t][:, :, cols], res[:, cols])

@@ -13,186 +13,228 @@ ALU = mybir.AluOpType
 ACT = mybir.ActivationFunctionType
 
 P = 128
-T, G, S = 1024, 2048, 512
+TOKENS = 1024
+CODEWORDS = 2048
+S = 512
 TILES = 4
-HALF = 256
-FUSED = ((0, 2), (0, 3), (1, 0), (1, 1))
-FLOPS = 3 * 2 * 512 * 512 * 512
+BLOCKS = 16
+ROWS = 8
+RUNS = 8
+GROUP = 16
+QUADRANT = 32
+HALF = S // 2
+SIXTEENTH = 0.0625
+
+FUSED_STEPS = range(2, 6)
+VECTOR_ALONE_STEP = 4
+SCALAR_W_TILES = 2
+
+FLOPS = 3 * 2 * S * S * S
 
 
-def tile_picked_twpqjointbrange_none_p_kernel(tc, x_words, x_scales, d_words, d_scales, gn, w1, offs, k1, two, k2, n1, n2, n3, n4, out):
+def tile_picked_twpqjointbrange_none_p_kernel(
+    tc, x_words, x_scales, d_words, d_scales, gn, w1, offs, k1, two, k2, n1, n2, n3, n4, out
+):
     nc = tc.nc
     with ExitStack() as ctx:
         sb = ctx.enter_context(tc.tile_pool(name="sb", bufs=1))
         ps = ctx.enter_context(tc.psum_pool(name="ps", bufs=1))
 
-        def tile(name, shape, dtype, tag=None):
-            return sb.tile(shape, dtype, name=name, tag=tag or name, align_bytes=64)
+        def tile(name, shape, dtype, reuses=None):
+            return sb.tile(shape, dtype, name=name, tag=reuses or name, align_bytes=64)
 
         def load_list(name, src):
-            t = sb.tile([P, S // 16], U16, name=name)
-            nc.sync.dma_start(t[:], src)
-            return t
+            entries = sb.tile([P, S // GROUP], U16, name=name)
+            nc.sync.dma_start(entries[:], src)
+            return entries
 
-        d_bytes = tile("d_bytes", [P, G], U8)
-        x_bytes = tile("x_bytes", [P, T], U8)
+        def load_words(name, src, columns):
+            table = tile(name, [P, columns], U32)
+            nc.sync.dma_start(table[:].bitcast(I32), src[0].rearrange("p n t -> p (n t)").bitcast(I32))
+            return table
 
+        d_bytes = tile("d_bytes", [P, CODEWORDS], U8)
+        x_bytes = tile("x_bytes", [P, TOKENS], U8)
         l_k2 = load_list("l_k2", k2)
         d_rows = d_scales[0].bitcast(I32).rearrange("(r e) c -> e r c", e=2)
         for e in range(2):
-            nc.sync.dma_start(d_bytes[e:P:2, :].bitcast(I32), d_rows[e].unsqueeze(1).to_broadcast([8, 8, G // 4]))
+            repeated = d_rows[e].unsqueeze(1).to_broadcast([RUNS, GROUP // 2, CODEWORDS // 4])
+            nc.sync.dma_start(d_bytes[e:P:2, :].bitcast(I32), repeated)
         l_two = load_list("l_two", two)
-        x_tab = tile("x_tab", [P, T], U32)
-        nc.sync.dma_start(x_tab[:].bitcast(I32), x_words[0].rearrange("p n t -> p (n t)").bitcast(I32))
-        x_rows = x_scales[0].bitcast(I32).rearrange("(q s) c -> q s c", s=4)
-        for q in range(4):
-            nc.sync.dma_start(x_bytes[32 * q:32 * (q + 1), :].bitcast(I32), x_rows[q].unsqueeze(0).to_broadcast([8, 4, T // 4]))
-        d_tab = tile("d_tab", [P, G], U32)
-        nc.sync.dma_start(d_tab[:].bitcast(I32), d_words[0].rearrange("p n t -> p (n t)").bitcast(I32))
+        x_table = load_words("x_table", x_words, TOKENS)
+        x_rows = x_scales[0].bitcast(I32).rearrange("(Q s) c -> Q s c", s=4)
+        for Q in range(P // QUADRANT):
+            repeated = x_rows[Q].unsqueeze(0).to_broadcast([QUADRANT // 4, 4, TOKENS // 4])
+            nc.sync.dma_start(x_bytes[QUADRANT * Q : QUADRANT * (Q + 1), :].bitcast(I32), repeated)
+        d_table = load_words("d_table", d_words, CODEWORDS)
 
-        def deal(dst, src, run):
-            nc.vector.tensor_copy(out=dst.rearrange("p (t b q) -> p t b q", t=TILES, q=run),
-                                  in_=src.rearrange("p (b t q) -> p t b q", t=TILES, q=run))
+        def deal(dst, src):
+            nc.vector.tensor_copy(
+                out=dst.rearrange("p (t B q) -> p t B q", t=TILES, B=BLOCKS),
+                in_=src.rearrange("p (B t q) -> p t B q", t=TILES, B=BLOCKS),
+            )
 
-        def pick_scales(name, codes, queue, tag):
-            got = tile(name + "_sg", [P, S], U8, tag)
-            nc.vector.tensor_copy(out=got[:], in_=d_bytes[:].indirect(codes[:]))
-            odd = tile(name + "_so", [P, S], U8)
-            plane = tile(name + "_sp", [P, S], U8)
-            deal(odd[:].bitcast(I32), got[:].bitcast(I32), 2)
-            deal(plane[:].bitcast(I32), got[:].bitcast(I32), 2)
+        def pick_codeword_plane(name, codes, queue):
+            picked = tile(name + "_picked_bytes", [P, S], U8)
+            nc.vector.tensor_copy(out=picked[:], in_=d_bytes[:].indirect(codes[:]))
+            odd_runs = tile(name + "_odd_runs", [P, S], U8)
+            plane = tile(name + "_plane", [P, S], U8)
+            deal(odd_runs[:].bitcast(I32), picked[:].bitcast(I32))
+            deal(plane[:].bitcast(I32), picked[:].bitcast(I32))
             for e in range(2):
-                queue.dma_start(plane[2 + e:P:32, :].bitcast(I32), odd[16 + e:P:32, :].bitcast(I32))
+                queue.dma_start(plane[2 + e : P : QUADRANT, :].bitcast(I32), odd_runs[GROUP + e : P : QUADRANT, :].bitcast(I32))
             return plane
 
-        def pick_words(name, codes):
-            got = tile(name + "_wg", [P, S], U32, "picked")
-            nc.vector.tensor_copy(out=got[:], in_=d_tab[:].indirect(codes[:]))
-            dealt = tile(name + "_wd", [P, S], U32)
-            deal(dealt[:], got[:], 8)
+        def pick_codeword_words(name, codes):
+            picked = tile(name + "_picked_words", [P, S], U32)
+            nc.vector.tensor_copy(out=picked[:], in_=d_table[:].indirect(codes[:]))
+            dealt = tile(name + "_words", [P, S], U32)
+            deal(dealt[:], picked[:])
             return dealt
 
-        def pick_token_words(name, tokens):
-            words = tile(name + "_xw", [P, S], U32, "token_words")
-            nc.vector.tensor_copy(out=words[:], in_=x_tab[:].indirect(tokens[:]))
-            return words
+        def pick_tokens(name, table, dtype, tokens):
+            picked = tile(name, [P, S], dtype)
+            nc.vector.tensor_copy(out=picked[:], in_=table[:].indirect(tokens[:]))
+            return picked
 
-        def pick_token_scales(name, tokens):
-            scales = tile(name + "_xs", [P, S], U8, "token_scales")
-            nc.vector.tensor_copy(out=scales[:], in_=x_bytes[:].indirect(tokens[:]))
-            return scales
+        def product(dst, t, row_words, row_plane, column_words, column_plane):
+            rows = slice(t * P, (t + 1) * P)
+            nc.tensor.matmul_mx(
+                out=dst,
+                lhsT=row_words[:, rows].bitcast(FP8X4),
+                lhsT_scale=row_plane[:, rows],
+                rhs=column_words[:].bitcast(FP8X4),
+                rhs_scale=column_plane[:],
+                start=True,
+                stop=True,
+            )
 
-        def product(dst, lw, ls, t, rw, rs):
-            cols = slice(t * P, (t + 1) * P)
-            nc.tensor.matmul_mx(out=dst, lhsT=lw[:, cols].bitcast(FP8X4), lhsT_scale=ls[:, cols],
-                                rhs=rw.bitcast(FP8X4), rhs_scale=rs, start=True, stop=True)
+        def gather_on_scalar(dst, window, entries):
+            nc.scalar.activation(out=dst, in_=window[:].indirect(entries), func=ACT.Copy)
 
-        b_ds = pick_scales("b", l_k2, nc.scalar, "b_sg")
-        b_xw = pick_token_words("b", l_two)
-        b_xs = pick_token_scales("b", l_two)
-        b_dw = pick_words("b", l_k2)
+        b_plane = pick_codeword_plane("b", l_k2, nc.scalar)
+        b_token_words = pick_tokens("b_token_words", x_table, U32, l_two)
+        b_token_plane = pick_tokens("b_token_plane", x_bytes, U8, l_two)
+        b_words = pick_codeword_words("b", l_k2)
 
         l_n1 = load_list("l_n1", n1)
-        l_n2 = load_list("l_n2", n2)
         l_k1 = load_list("l_k1", k1)
+        l_n2 = load_list("l_n2", n2)
         l_offs = load_list("l_offs", offs)
-        w_raw = tile("w_raw", [P, TILES, S], F32)
-        w_rows = w1.rearrange("(b j q) c -> j b q c", j=TILES, q=8)
-        for j in range(TILES):
-            nc.sync.dma_start(w_raw[:, j, :], w_rows[j])
+
+        b = []
+        for t in range(TILES):
+            bank = ps.tile([P, S], F32, name=f"b_bank{t}", tag=f"bank{t}")
+            product(bank[:], t, b_words, b_plane, b_token_words, b_token_plane)
+            b.append(tile(f"b{t}", [P, S], F32))
+            nc.scalar.activation(out=b[t][:], in_=bank[:], func=ACT.Copy, scale=SIXTEENTH)
+
+        a_plane = pick_codeword_plane("a", l_k1, nc.sync)
+        a_words = pick_codeword_words("a", l_k1)
+        a_token_words = pick_tokens("a_token_words", x_table, U32, l_offs)
+        a_token_plane = pick_tokens("a_token_plane", x_bytes, U8, l_offs)
+
         gain = tile("gain", [P, TILES, 8], F32)
-        g_rows = gn.rearrange("(b j q) o -> j b q o", j=TILES, q=8)
-        for j in range(TILES):
-            nc.sync.dma_start(gain[:, j, 0:1], g_rows[j])
+        gn_rows = gn.rearrange("(B t q) o -> t B q o", t=TILES, q=ROWS)
+        for t in range(TILES):
+            nc.sync.dma_start(gain[:, t, 0:1], gn_rows[t])
+        w_raw = tile("w_raw", [P, TILES, S], F32)
+        w_rows = w1.rearrange("(B t q) m -> t B q m", t=TILES, q=ROWS)
+        for t in range(TILES):
+            nc.sync.dma_start(w_raw[:, t, :], w_rows[t])
         l_n3 = load_list("l_n3", n3)
         l_n4 = load_list("l_n4", n4)
 
-        b_win = []
+        a_banks = []
         for t in range(TILES):
-            bank = ps.tile([P, S], F32, name=f"b_ps{t}", tag=f"bank{t}")
-            product(bank[:], b_dw, b_ds, t, b_xw[:], b_xs[:])
-            win = tile(f"b_win{t}", [P, S], F32)
-            nc.scalar.activation(out=win[:], in_=bank[:], func=ACT.Copy, scale=0.0625)
-            b_win.append(win)
-
-        a_ds = pick_scales("a", l_k1, nc.sync, "picked")
-        a_dw = pick_words("a", l_k1)
-        a_xw = pick_token_words("a", l_offs)
-        a_xs = pick_token_scales("a", l_offs)
-        a_ps = []
-        for t in range(TILES):
-            bank = ps.tile([P, S], F32, name=f"a_ps{t}", tag=f"bank{TILES + t}")
-            product(bank[:], a_dw, a_ds, t, a_xw[:], a_xs[:])
-            a_ps.append(bank)
-
+            a_banks.append(ps.tile([P, S], F32, name=f"a_bank{t}", tag=f"bank{TILES + t}"))
+            product(a_banks[t][:], t, a_words, a_plane, a_token_words, a_token_plane)
         gain16 = tile("gain16", [P, TILES], F32)
-        nc.vector.tensor_scalar(out=gain16[:], in0=gain[:, :, 0], scalar1=0.0625, scalar2=None, op0=ALU.mult)
+        nc.vector.tensor_scalar(out=gain16[:], in0=gain[:, :, 0], scalar1=SIXTEENTH, scalar2=None, op0=ALU.mult)
 
-        def offsets(lst, c):
-            return lst[:, c * HALF // 16:(c + 1) * HALF // 16]
-
-        z_q = []
-        for c in range(2):
-            cols = slice(c * HALF, (c + 1) * HALF)
-            z_rows = tile(f"z_rows{c}", [P, TILES, HALF], BF16)
+        z_halves = []
+        for half in range(2):
+            cols = slice(half * HALF, (half + 1) * HALF)
+            entries = slice(cols.start // GROUP, cols.stop // GROUP)
+            z_rows = tile(f"z_rows{half}", [P, TILES, HALF], BF16)
             for t in range(TILES):
-                first = tile(f"first{c}_{t}", [P, HALF], F32)
-                diff = sb.tile([P, HALF], F32, name=f"diff{c}_{t}", tag=f"diff{c}_{t}", align_bytes=64)
-                nc.scalar.activation(out=first[:], in_=b_win[t][:].indirect(offsets(l_n1, c)), func=ACT.Copy)
-                if (c, t) not in FUSED:
-                    second = tile(f"second{c}_{t}", [P, HALF], F32)
-                    nc.scalar.activation(out=second[:], in_=b_win[t][:].indirect(offsets(l_n2, c)), func=ACT.Copy)
-                    nc.vector.tensor_tensor(out=diff[:], in0=second[:], in1=first[:], op=ALU.subtract)
+                step = TILES * half + t
+                at_n1 = tile(f"at_n1_{step}", [P, HALF], F32)
+                diff = tile(f"diff{step}", [P, HALF], F32)
+                if step == VECTOR_ALONE_STEP:
+                    nc.vector.tensor_copy(out=at_n1[:], in_=b[t][:].indirect(l_n1[:, entries]))
                 else:
-                    nc.vector.tensor_tensor(out=diff[:], in0=b_win[t][:].indirect(offsets(l_n2, c)), in1=first[:], op=ALU.subtract)
-                th = tile(f"th{c}_{t}", [P, HALF], F32)
-                nc.scalar.activation(out=th[:], in_=diff[:], func=ACT.Tanh, scale=-1.0)
-                nc.vector.scalar_tensor_tensor(out=z_rows[:, t, :], in0=a_ps[t][:, cols], scalar=gain16[:, t:t + 1], in1=th[:],
-                                               op0=ALU.mult, op1=ALU.mult)
-            z_bf = tile(f"z_bf{c}", [P, HALF, TILES], BF16)
-            nc.vector.tensor_copy(out=z_bf[:].rearrange("p (c i) t -> p c t i", i=4), in_=z_rows[:].rearrange("p t (c i) -> p c t i", i=4))
-            z_codes = tile(f"z_codes{c}", [P, HALF], U32)
-            z_plane = tile(f"z_plane{c}", [P, HALF], U8)
-            nc.vector.quantize_mx(out=z_codes[:].bitcast(FP8X4), scales=z_plane[:], in_=z_bf[:].rearrange("p j t -> p (j t)"))
-            z_q.append((z_codes, z_plane))
+                    gather_on_scalar(at_n1[:], b[t], l_n1[:, entries])
+                if step in FUSED_STEPS:
+                    nc.vector.tensor_tensor(out=diff[:], in0=b[t][:].indirect(l_n2[:, entries]), in1=at_n1[:], op=ALU.subtract)
+                else:
+                    at_n2 = tile(f"at_n2_{step}", [P, HALF], F32)
+                    gather_on_scalar(at_n2[:], b[t], l_n2[:, entries])
+                    subtracter = nc.gpsimd if half == 0 else nc.vector
+                    subtracter.tensor_tensor(out=diff[:], in0=at_n2[:], in1=at_n1[:], op=ALU.subtract)
+                gate = tile(f"gate{step}", [P, HALF], F32)
+                nc.scalar.activation(out=gate[:], in_=diff[:], func=ACT.Tanh, scale=-1.0)
+                nc.vector.scalar_tensor_tensor(
+                    out=z_rows[:, t, :], in0=a_banks[t][:, cols], scalar=gain16[:, t : t + 1], in1=gate[:], op0=ALU.mult, op1=ALU.mult
+                )
+            z_side = tile(f"z_side{half}", [P, HALF, TILES], BF16)
+            nc.vector.tensor_copy(
+                out=z_side[:].rearrange("p (c i) t -> p c t i", i=4), in_=z_rows[:].rearrange("p t (c i) -> p c t i", i=4)
+            )
+            z_words = tile(f"z_words{half}", [P, HALF], U32)
+            z_plane = tile(f"z_plane{half}", [P, HALF], U8)
+            nc.vector.quantize_mx(out=z_words[:].bitcast(FP8X4), scales=z_plane[:], in_=z_side[:].rearrange("p j t -> p (j t)"))
+            z_halves.append((z_words, z_plane))
 
-        w_bf = sb.tile([P, TILES, 16, 8, 4], BF16, name="w_bf", tag="diff1_3", align_bytes=64)
-        w_view = w_raw[:].rearrange("p j (b t q) -> p t b q j", t=TILES, q=8)
-        w_codes = tile("w_codes", [P, S], U32)
+        w_view = w_raw[:].rearrange("p u (B t q) -> p t B q u", t=TILES, q=ROWS)
+        w_words = tile("w_words", [P, S], U32)
         w_plane = tile("w_plane", [P, S], U8)
-        out_rows = out.rearrange("(b t q) j -> t b q j", t=TILES, q=8)
-        h_ps, h_win = [], []
-        for t in range(TILES):
+        w_first = tile("w_first", [P, SCALAR_W_TILES, BLOCKS, ROWS, TILES], BF16, reuses=f"diff{2 * TILES - 1}")
+        for t in range(SCALAR_W_TILES):
             rows = slice(t * P, (t + 1) * P)
-            nc.scalar.copy(out=w_bf[:, t], in_=w_view[:, t])
-            nc.vector.quantize_mx(out=w_codes[:, rows].bitcast(FP8X4), scales=w_plane[:, rows], in_=w_bf[:, t].rearrange("p b q j -> p (b q j)"))
-            bank = ps.tile([P, S], F32, name=f"h_ps{t}", tag=f"bank{t}")
-            for c in range(2):
-                product(bank[:, c * HALF:(c + 1) * HALF], w_codes, w_plane, t, z_q[c][0][:], z_q[c][1][:])
-            h_ps.append(bank)
+            nc.scalar.copy(out=w_first[:, t], in_=w_view[:, t])
+            nc.vector.quantize_mx(
+                out=w_words[:, rows].bitcast(FP8X4), scales=w_plane[:, rows], in_=w_first[:, t].rearrange("p B q u -> p (B q u)")
+            )
+        rest = slice(SCALAR_W_TILES * P, S)
+        w_rest = tile("w_rest", [P, TILES - SCALAR_W_TILES, BLOCKS, ROWS, TILES], BF16, reuses="z_side1")
+        nc.vector.tensor_copy(out=w_rest[:], in_=w_view[:, SCALAR_W_TILES:TILES])
+        nc.vector.quantize_mx(
+            out=w_words[:, rest].bitcast(FP8X4), scales=w_plane[:, rest], in_=w_rest[:].rearrange("p t B q u -> p (t B q u)")
+        )
 
+        h_banks = []
         for t in range(TILES):
-            win = tile(f"h_win{t}", [P, 2 * S], F32)
-            nc.scalar.activation(out=win[:, 0:S], in_=h_ps[t][:], func=ACT.Copy, scale=0.5)
-            h_win.append(win)
-            pa = tile(f"pa{t}", [P, S], F32)
-            pb = tile(f"pb{t}", [P, S], F32)
+            h_banks.append(ps.tile([P, S], F32, name=f"h_bank{t}", tag=f"bank{t}"))
+            for half, (z_words, z_plane) in enumerate(z_halves):
+                product(h_banks[t][:, half * HALF : (half + 1) * HALF], t, w_words, w_plane, z_words, z_plane)
+
+        out_rows = out.rearrange("(B t q) j -> t B q j", t=TILES, q=ROWS)
+        for t in range(TILES):
+            last = t == TILES - 1
+            h_half = tile(f"h_half{t}", [P, 2 * S], F32)
+            nc.scalar.activation(out=h_half[:, 0:S], in_=h_banks[t][:], func=ACT.Copy, scale=0.5)
+            pa_half = tile(f"pa_half{t}", [P, S], F32)
+            pb_half = tile(f"pb_half{t}", [P, S], F32)
             if t == 0:
-                nc.vector.tensor_copy(out=pa[:], in_=h_win[t][:].indirect(l_n3[:]))
+                nc.vector.tensor_copy(out=pa_half[:], in_=h_half[:].indirect(l_n3[:]))
             else:
-                nc.scalar.activation(out=pa[:], in_=h_win[t][:].indirect(l_n3[:]), func=ACT.Copy)
-            pieces = [slice(0, S)] if t < TILES - 1 else [slice(0, HALF), slice(HALF, S)]
+                gather_on_scalar(pa_half[:], h_half, l_n3[:])
+            pieces = [slice(0, HALF), slice(HALF, S)] if last else [slice(0, S)]
             for cols in pieces:
-                nc.scalar.activation(out=pb[:, cols], in_=h_win[t][:].indirect(l_n4[:, cols.start // 16:cols.stop // 16]), func=ACT.Copy)
-            hi = tile(f"hi{t}", [P, S], F32)
-            lo = tile(f"lo{t}", [P, S], F32)
-            top = tile(f"top{t}", [P, S], F32)
-            low = tile(f"low{t}", [P, S], F32)
-            res = tile(f"res{t}", [P, S], F32)
-            nc.vector.scalar_tensor_tensor(out=hi[:], in0=pa[:], scalar=2.0, in1=h_ps[t][:], op0=ALU.mult, op1=ALU.max)
-            nc.vector.scalar_tensor_tensor(out=lo[:], in0=h_ps[t][:], scalar=0.5, in1=pa[:], op0=ALU.mult, op1=ALU.min)
+                gather_on_scalar(pb_half[:, cols], h_half, l_n4[:, cols.start // GROUP : cols.stop // GROUP])
+            max2 = tile(f"max2_{t}", [P, S], F32)
+            min2_half = tile(f"min2_half{t}", [P, S], F32)
+            max3 = tile(f"max3_{t}", [P, S], F32)
+            min3_half = tile(f"min3_half{t}", [P, S], F32)
+            result = tile(f"result{t}", [P, S], F32)
+            nc.vector.scalar_tensor_tensor(out=max2[:], in0=pa_half[:], scalar=2.0, in1=h_banks[t][:], op0=ALU.mult, op1=ALU.max)
+            nc.vector.scalar_tensor_tensor(out=min2_half[:], in0=h_banks[t][:], scalar=0.5, in1=pa_half[:], op0=ALU.mult, op1=ALU.min)
             for cols in pieces:
-                nc.vector.scalar_tensor_tensor(out=top[:, cols], in0=pb[:, cols], scalar=2.0, in1=hi[:, cols], op0=ALU.mult, op1=ALU.max)
-                nc.vector.tensor_tensor(out=low[:, cols], in0=pb[:, cols], in1=lo[:, cols], op=ALU.min)
-                nc.vector.tensor_tensor(out=res[:, cols], in0=top[:, cols], in1=low[:, cols], op=ALU.subtract)
-                nc.sync.dma_start(out_rows[t][:, :, cols], res[:, cols])
+                nc.vector.scalar_tensor_tensor(
+                    out=max3[:, cols], in0=pb_half[:, cols], scalar=2.0, in1=max2[:, cols], op0=ALU.mult, op1=ALU.max
+                )
+                nc.vector.tensor_tensor(out=min3_half[:, cols], in0=pb_half[:, cols], in1=min2_half[:, cols], op=ALU.min)
+                subtracter = nc.vector if last else nc.gpsimd
+                subtracter.tensor_tensor(out=result[:, cols], in0=max3[:, cols], in1=min3_half[:, cols], op=ALU.subtract)
+                nc.sync.dma_start(out_rows[t][:, :, cols], result[:, cols])

from contextlib import ExitStack

import concourse.mybir as mybir

F32 = mybir.dt.float32
BF16 = mybir.dt.bfloat16
I32 = mybir.dt.int32
U32 = mybir.dt.uint32
U16 = mybir.dt.uint16
U8 = mybir.dt.uint8
FP8X4 = mybir.dt.float8_e4m3fn_x4
ALU = mybir.AluOpType
ACT = mybir.ActivationFunctionType

P = 128
TOKENS = 1024
CODEWORDS = 2048
S = 512
TILES = 4
BLOCKS = 16
ROWS = 8
RUNS = 8
GROUP = 16
QUADRANT = 32
HALF = S // 2
SIXTEENTH = 0.0625

FUSED_STEPS = range(2, 6)
VECTOR_ALONE_STEP = 4
SCALAR_W_TILES = 2

FLOPS = 3 * 2 * S * S * S


def tile_picked_twpqjointbrange_none_p_kernel(
    tc, x_words, x_scales, d_words, d_scales, gn, w1, offs, k1, two, k2, n1, n2, n3, n4, out
):
    nc = tc.nc
    with ExitStack() as ctx:
        sb = ctx.enter_context(tc.tile_pool(name="sb", bufs=1))
        ps = ctx.enter_context(tc.psum_pool(name="ps", bufs=1))

        def tile(name, shape, dtype, reuses=None):
            return sb.tile(shape, dtype, name=name, tag=reuses or name, align_bytes=64)

        def load_list(name, src):
            entries = sb.tile([P, S // GROUP], U16, name=name)
            nc.sync.dma_start(entries[:], src)
            return entries

        def load_words(name, src, columns):
            table = tile(name, [P, columns], U32)
            nc.sync.dma_start(table[:].bitcast(I32), src[0].rearrange("p n t -> p (n t)").bitcast(I32))
            return table

        d_bytes = tile("d_bytes", [P, CODEWORDS], U8)
        x_bytes = tile("x_bytes", [P, TOKENS], U8)
        l_k2 = load_list("l_k2", k2)
        d_rows = d_scales[0].bitcast(I32).rearrange("(r e) c -> e r c", e=2)
        for e in range(2):
            repeated = d_rows[e].unsqueeze(1).to_broadcast([RUNS, GROUP // 2, CODEWORDS // 4])
            nc.sync.dma_start(d_bytes[e:P:2, :].bitcast(I32), repeated)
        l_two = load_list("l_two", two)
        x_table = load_words("x_table", x_words, TOKENS)
        x_rows = x_scales[0].bitcast(I32).rearrange("(Q s) c -> Q s c", s=4)
        for Q in range(P // QUADRANT):
            repeated = x_rows[Q].unsqueeze(0).to_broadcast([QUADRANT // 4, 4, TOKENS // 4])
            nc.sync.dma_start(x_bytes[QUADRANT * Q : QUADRANT * (Q + 1), :].bitcast(I32), repeated)
        d_table = load_words("d_table", d_words, CODEWORDS)

        def deal(dst, src):
            nc.vector.tensor_copy(
                out=dst.rearrange("p (t B q) -> p t B q", t=TILES, B=BLOCKS),
                in_=src.rearrange("p (B t q) -> p t B q", t=TILES, B=BLOCKS),
            )

        def pick_codeword_plane(name, codes, queue):
            picked = tile(name + "_picked_bytes", [P, S], U8)
            nc.vector.tensor_copy(out=picked[:], in_=d_bytes[:].indirect(codes[:]))
            odd_runs = tile(name + "_odd_runs", [P, S], U8)
            plane = tile(name + "_plane", [P, S], U8)
            deal(odd_runs[:].bitcast(I32), picked[:].bitcast(I32))
            deal(plane[:].bitcast(I32), picked[:].bitcast(I32))
            for e in range(2):
                queue.dma_start(plane[2 + e : P : QUADRANT, :].bitcast(I32), odd_runs[GROUP + e : P : QUADRANT, :].bitcast(I32))
            return plane

        def pick_codeword_words(name, codes):
            picked = tile(name + "_picked_words", [P, S], U32)
            nc.vector.tensor_copy(out=picked[:], in_=d_table[:].indirect(codes[:]))
            dealt = tile(name + "_words", [P, S], U32)
            deal(dealt[:], picked[:])
            return dealt

        def pick_tokens(name, table, dtype, tokens):
            picked = tile(name, [P, S], dtype)
            nc.vector.tensor_copy(out=picked[:], in_=table[:].indirect(tokens[:]))
            return picked

        def product(dst, t, row_words, row_plane, column_words, column_plane):
            rows = slice(t * P, (t + 1) * P)
            nc.tensor.matmul_mx(
                out=dst,
                lhsT=row_words[:, rows].bitcast(FP8X4),
                lhsT_scale=row_plane[:, rows],
                rhs=column_words[:].bitcast(FP8X4),
                rhs_scale=column_plane[:],
                start=True,
                stop=True,
            )

        def gather_on_scalar(dst, window, entries):
            nc.scalar.activation(out=dst, in_=window[:].indirect(entries), func=ACT.Copy)

        b_plane = pick_codeword_plane("b", l_k2, nc.scalar)
        b_token_words = pick_tokens("b_token_words", x_table, U32, l_two)
        b_token_plane = pick_tokens("b_token_plane", x_bytes, U8, l_two)
        b_words = pick_codeword_words("b", l_k2)

        l_n1 = load_list("l_n1", n1)
        l_k1 = load_list("l_k1", k1)
        l_n2 = load_list("l_n2", n2)
        l_offs = load_list("l_offs", offs)

        b = []
        for t in range(TILES):
            bank = ps.tile([P, S], F32, name=f"b_bank{t}", tag=f"bank{t}")
            product(bank[:], t, b_words, b_plane, b_token_words, b_token_plane)
            b.append(tile(f"b{t}", [P, S], F32))
            nc.scalar.activation(out=b[t][:], in_=bank[:], func=ACT.Copy, scale=SIXTEENTH)

        a_plane = pick_codeword_plane("a", l_k1, nc.sync)
        a_words = pick_codeword_words("a", l_k1)
        a_token_words = pick_tokens("a_token_words", x_table, U32, l_offs)
        a_token_plane = pick_tokens("a_token_plane", x_bytes, U8, l_offs)

        gain = tile("gain", [P, TILES, 8], F32)
        gn_rows = gn.rearrange("(B t q) o -> t B q o", t=TILES, q=ROWS)
        for t in range(TILES):
            nc.sync.dma_start(gain[:, t, 0:1], gn_rows[t])
        w_raw = tile("w_raw", [P, TILES, S], F32)
        w_rows = w1.rearrange("(B t q) m -> t B q m", t=TILES, q=ROWS)
        for t in range(TILES):
            nc.sync.dma_start(w_raw[:, t, :], w_rows[t])
        l_n3 = load_list("l_n3", n3)
        l_n4 = load_list("l_n4", n4)

        a_banks = []
        for t in range(TILES):
            a_banks.append(ps.tile([P, S], F32, name=f"a_bank{t}", tag=f"bank{TILES + t}"))
            product(a_banks[t][:], t, a_words, a_plane, a_token_words, a_token_plane)
        gain16 = tile("gain16", [P, TILES], F32)
        nc.vector.tensor_scalar(out=gain16[:], in0=gain[:, :, 0], scalar1=SIXTEENTH, scalar2=None, op0=ALU.mult)

        z_halves = []
        for half in range(2):
            cols = slice(half * HALF, (half + 1) * HALF)
            entries = slice(cols.start // GROUP, cols.stop // GROUP)
            z_rows = tile(f"z_rows{half}", [P, TILES, HALF], BF16)
            for t in range(TILES):
                step = TILES * half + t
                at_n1 = tile(f"at_n1_{step}", [P, HALF], F32)
                diff = tile(f"diff{step}", [P, HALF], F32)
                if step == VECTOR_ALONE_STEP:
                    nc.vector.tensor_copy(out=at_n1[:], in_=b[t][:].indirect(l_n1[:, entries]))
                else:
                    gather_on_scalar(at_n1[:], b[t], l_n1[:, entries])
                if step in FUSED_STEPS:
                    nc.vector.tensor_tensor(out=diff[:], in0=b[t][:].indirect(l_n2[:, entries]), in1=at_n1[:], op=ALU.subtract)
                else:
                    at_n2 = tile(f"at_n2_{step}", [P, HALF], F32)
                    gather_on_scalar(at_n2[:], b[t], l_n2[:, entries])
                    subtracter = nc.gpsimd if half == 0 else nc.vector
                    subtracter.tensor_tensor(out=diff[:], in0=at_n2[:], in1=at_n1[:], op=ALU.subtract)
                gate = tile(f"gate{step}", [P, HALF], F32)
                nc.scalar.activation(out=gate[:], in_=diff[:], func=ACT.Tanh, scale=-1.0)
                nc.vector.scalar_tensor_tensor(
                    out=z_rows[:, t, :], in0=a_banks[t][:, cols], scalar=gain16[:, t : t + 1], in1=gate[:], op0=ALU.mult, op1=ALU.mult
                )
            z_side = tile(f"z_side{half}", [P, HALF, TILES], BF16)
            nc.vector.tensor_copy(
                out=z_side[:].rearrange("p (c i) t -> p c t i", i=4), in_=z_rows[:].rearrange("p t (c i) -> p c t i", i=4)
            )
            z_words = tile(f"z_words{half}", [P, HALF], U32)
            z_plane = tile(f"z_plane{half}", [P, HALF], U8)
            nc.vector.quantize_mx(out=z_words[:].bitcast(FP8X4), scales=z_plane[:], in_=z_side[:].rearrange("p j t -> p (j t)"))
            z_halves.append((z_words, z_plane))

        w_view = w_raw[:].rearrange("p u (B t q) -> p t B q u", t=TILES, q=ROWS)
        w_words = tile("w_words", [P, S], U32)
        w_plane = tile("w_plane", [P, S], U8)
        w_first = tile("w_first", [P, SCALAR_W_TILES, BLOCKS, ROWS, TILES], BF16, reuses=f"diff{2 * TILES - 1}")
        for t in range(SCALAR_W_TILES):
            rows = slice(t * P, (t + 1) * P)
            nc.scalar.copy(out=w_first[:, t], in_=w_view[:, t])
            nc.vector.quantize_mx(
                out=w_words[:, rows].bitcast(FP8X4), scales=w_plane[:, rows], in_=w_first[:, t].rearrange("p B q u -> p (B q u)")
            )
        rest = slice(SCALAR_W_TILES * P, S)
        w_rest = tile("w_rest", [P, TILES - SCALAR_W_TILES, BLOCKS, ROWS, TILES], BF16, reuses="z_side1")
        nc.vector.tensor_copy(out=w_rest[:], in_=w_view[:, SCALAR_W_TILES:TILES])
        nc.vector.quantize_mx(
            out=w_words[:, rest].bitcast(FP8X4), scales=w_plane[:, rest], in_=w_rest[:].rearrange("p t B q u -> p (t B q u)")
        )

        h_banks = []
        for t in range(TILES):
            h_banks.append(ps.tile([P, S], F32, name=f"h_bank{t}", tag=f"bank{t}"))
            for half, (z_words, z_plane) in enumerate(z_halves):
                product(h_banks[t][:, half * HALF : (half + 1) * HALF], t, w_words, w_plane, z_words, z_plane)

        out_rows = out.rearrange("(B t q) j -> t B q j", t=TILES, q=ROWS)
        for t in range(TILES):
            last = t == TILES - 1
            h_half = tile(f"h_half{t}", [P, 2 * S], F32)
            nc.scalar.activation(out=h_half[:, 0:S], in_=h_banks[t][:], func=ACT.Copy, scale=0.5)
            pa_half = tile(f"pa_half{t}", [P, S], F32)
            pb_half = tile(f"pb_half{t}", [P, S], F32)
            if t == 0:
                nc.vector.tensor_copy(out=pa_half[:], in_=h_half[:].indirect(l_n3[:]))
            else:
                gather_on_scalar(pa_half[:], h_half, l_n3[:])
            pieces = [slice(0, HALF), slice(HALF, S)] if last else [slice(0, S)]
            for cols in pieces:
                gather_on_scalar(pb_half[:, cols], h_half, l_n4[:, cols.start // GROUP : cols.stop // GROUP])
            max2 = tile(f"max2_{t}", [P, S], F32)
            min2_half = tile(f"min2_half{t}", [P, S], F32)
            max3 = tile(f"max3_{t}", [P, S], F32)
            min3_half = tile(f"min3_half{t}", [P, S], F32)
            result = tile(f"result{t}", [P, S], F32)
            nc.vector.scalar_tensor_tensor(out=max2[:], in0=pa_half[:], scalar=2.0, in1=h_banks[t][:], op0=ALU.mult, op1=ALU.max)
            nc.vector.scalar_tensor_tensor(out=min2_half[:], in0=h_banks[t][:], scalar=0.5, in1=pa_half[:], op0=ALU.mult, op1=ALU.min)
            for cols in pieces:
                nc.vector.scalar_tensor_tensor(
                    out=max3[:, cols], in0=pb_half[:, cols], scalar=2.0, in1=max2[:, cols], op0=ALU.mult, op1=ALU.max
                )
                nc.vector.tensor_tensor(out=min3_half[:, cols], in0=pb_half[:, cols], in1=min2_half[:, cols], op=ALU.min)
                subtracter = nc.vector if last else nc.gpsimd
                subtracter.tensor_tensor(out=result[:, cols], in0=max3[:, cols], in1=min3_half[:, cols], op=ALU.subtract)
                nc.sync.dma_start(out_rows[t][:, :, cols], result[:, cols])
